import numpy as np
import ml_dtypes


def mxq(x, axis, fmt="e4m3"):
    dtype, down = {"e4m3": (ml_dtypes.float8_e4m3fn, 7), "e5m2": (ml_dtypes.float8_e5m2, 14)}[fmt]
    v = np.moveaxis(np.asarray(x, np.float32).astype(ml_dtypes.bfloat16).astype(np.float64), axis, -1)
    blocks = v.reshape(v.shape[:-1] + (-1, 32))
    amax = np.abs(blocks).max(-1, keepdims=True)
    byte = np.maximum(np.where(amax > 0, np.frexp(amax)[1] - 1 + 127, 0) - down, 1)
    scale = np.exp2(byte - 127.0)
    codes = (blocks / scale).astype(np.float32).astype(dtype).astype(np.float64)
    return np.moveaxis((codes * scale).reshape(v.shape), -1, axis)


WIDE = False


def mx_kscale(k):
    if not WIDE:
        return np.ones(k)
    levels = np.array([10, -10, 5, -5, 0])
    if k % 512:
        return np.exp2(np.random.permutation(np.resize(levels, k // 32))).repeat(32)
    a = np.empty((k // 512, 16))
    for p in range(k // 512):
        a[p, :8] = np.random.permutation(np.resize(levels, 8))
        for g in range(8):
            far = levels[np.abs(levels - a[p, g]) >= 10]
            a[p, g + 8] = far[np.random.randint(len(far))]
    return np.exp2(a.ravel()).repeat(32)


def f64(x):
    return np.asarray(x).astype(np.float64)


def striped(idx):
    return np.tile(idx.reshape(-1, 16).T, (8, 1)).astype(np.uint16)


def unstriped(offs):
    return offs[:16].T.reshape(-1).astype(np.int64)


E2M1 = np.array([0.0, 0.5, 1.0, 1.5, 2.0, 3.0, 4.0, 6.0, -0.0, -0.5, -1.0, -1.5, -2.0, -3.0, -4.0, -6.0])


def pack_weight(w, fmt):
    k, n = w.shape
    w = f64(np.asarray(w, np.float32).astype(ml_dtypes.bfloat16)).reshape(k // 32, 32, n)
    amax = np.abs(w).max(1)
    if fmt == "e4m3":
        byte = np.frexp(amax)[1] - 1 + 127 - 7
    else:
        mant, ex = np.frexp(amax / 6.0)
        byte = np.where(mant > 0.5, ex, ex - 1) + 127
    byte = np.clip(np.where(amax > 0, byte, 1), 1, 254)
    scaled = (w * np.exp2(127.0 - byte)[:, None, :]).reshape(k, n).astype(np.float32)
    by_word = np.ascontiguousarray(scaled.reshape(k // 512, 128, 4, n).transpose(0, 1, 3, 2))
    if fmt == "e4m3":
        words = by_word.astype(ml_dtypes.float8_e4m3fn).view(np.uint8)
    else:
        c = by_word.astype(ml_dtypes.float4_e2m1fn).view(np.uint8) & 0xF
        words = (c[..., 0::2] | (c[..., 1::2] << 4)).reshape(k // 512, 128, 2 * n)
    return np.ascontiguousarray(words), np.ascontiguousarray(byte.astype(np.uint8).reshape(k // 512, 16, n))


def unpack_weight(words, scales, fmt):
    g, _, n = scales.shape
    words = np.ascontiguousarray(words).reshape(g, 128, n, -1)
    if fmt == "e4m3":
        vals = words.view(ml_dtypes.float8_e4m3fn).astype(np.float64)
    else:
        nib = np.empty((g, 128, n, 4), np.uint8)
        nib[..., 0::2] = words & 0xF
        nib[..., 1::2] = words >> 4
        vals = E2M1[nib]
    vals = vals * np.repeat(np.exp2(scales.astype(np.float64) - 127.0), 8, axis=1)[..., None]
    return vals.transpose(0, 1, 3, 2).reshape(g * 512, n)


def gelu(v):
    return 0.5 * v * (1.0 + np.tanh(np.sqrt(2.0 / np.pi) * (v + 0.044715 * v**3)))


K, H, N, T, S, T2, P = 512, 1024, 512, 4096, 1024, 2048, 1024

def setup_inputs():
    n = np.random.standard_normal
    s = mx_kscale(K)[:, None]
    u = mx_kscale(H)[:, None]
    tab_words, tab_scales = pack_weight(n((K, T)) * s, "e4m3")
    w2_words, w2_scales = pack_weight(n((K, H)) / np.sqrt(K) / s * u.T, "e2m1")
    w4_words, w4_scales = pack_weight(n((H, N)) / np.sqrt(H) / u, "e2m1")
    return {
        "tab_words": tab_words, "tab_scales": tab_scales,
        "offs": striped(np.random.permutation(T)[:S]),
        "offs2": striped(np.random.permutation(T2)[:S]),
        "offs3": striped(np.random.permutation(T2)[:P]),
        "w1": (n((K, H)) / np.sqrt(K) / s * u.T).astype(np.float32),
        "w2_words": w2_words, "w2_scales": w2_scales,
        "gain": np.exp(0.4 * n(H)).astype(np.float32),
        "page0": (n((H, T2)) * u).astype(np.float32),
        "w3": (n((H, N)) / np.sqrt(H) / u).astype(np.float32),
        "w4_words": w4_words, "w4_scales": w4_scales,
        "w5": (n((K, N)) / np.sqrt(K) / s).astype(np.float32),
    }

def reference(tab_words, tab_scales, offs, offs2, offs3, w1, w2_words, w2_scales, gain, page0, w3, w4_words, w4_scales, w5):
    v = unpack_weight(tab_words, tab_scales, "e4m3")[:, unstriped(offs)]
    h1 = mxq(f64(w1), 0, "e4m3").T @ v
    h2 = unpack_weight(w2_words, w2_scales, "e2m1").T @ v
    page = f64(page0).copy()
    l2 = unstriped(offs2)
    page[:, l2] = np.maximum(page[:, l2] + h1, f64(gain)[:, None] * h2)
    x = mxq(page[:, unstriped(offs3)], 0, "e4m3")
    ya = mxq(f64(w3), 0, "e4m3").T @ x
    yb = unpack_weight(w4_words, w4_scales, "e2m1").T @ x
    skip = mxq(f64(w5), 0, "e4m3").T @ v
    return np.maximum(ya, yb) + skip

@@ -1,0 +1,307 @@
+from contextlib import ExitStack
+
+import concourse.mybir as mybir
+
+K, H, N, T, S, T2 = 512, 1024, 512, 4096, 1024, 2048
+FLOPS = 2 * S * (2 * K * H + 2 * H * N + K * N)
+
+F32 = mybir.dt.float32
+BF16 = mybir.dt.bfloat16
+I32 = mybir.dt.int32
+U32 = mybir.dt.uint32
+U16 = mybir.dt.uint16
+U8 = mybir.dt.uint8
+FP8X4 = mybir.dt.float8_e4m3fn_x4
+FP4X4 = mybir.dt.float4_e2m1fn_x4
+ADD = mybir.AluOpType.add
+MAX = mybir.AluOpType.max
+COPY = mybir.ActivationFunctionType.Copy
+
+P = 128
+PACK = 4
+KP = P * PACK
+BANK = 512
+SLICES = H // P
+CHUNK = 256
+CHUNKS = S // CHUNK
+PER_COL = 16
+
+
+def tile_list_building_tag_features_kernel(
+    tc, tab_words, tab_scales, offs, offs2, offs3, w1, w2_words, w2_scales, gain, page0, w3, w4_words, w4_scales, w5, out
+):
+    nc = tc.nc
+    with ExitStack() as ctx:
+        lists = ctx.enter_context(tc.tile_pool(name="lists", bufs=1))
+        held = ctx.enter_context(tc.tile_pool(name="held", bufs=1))
+        ring = ctx.enter_context(tc.tile_pool(name="ring", bufs=2))
+        psum = ctx.enter_context(tc.psum_pool(name="psum", bufs=1))
+
+        def bank(b):
+            return psum.tile([P, BANK], F32, name="bank%d" % b, tag="bank%d" % b)
+
+        def load_scale_rows(queue, plane, rows):
+            for q in range(4):
+                queue.dma_start(out=plane[32 * q : 32 * q + 4].bitcast(I32), in_=rows(q).bitcast(I32))
+
+        list1 = lists.tile([P, S // PER_COL], U16, name="list1")
+        list2 = lists.tile([P, S // PER_COL], U16, name="list2")
+        list3 = lists.tile([P, S // PER_COL], U16, name="list3")
+
+        tab_w = held.tile([P, T], I32, name="tab_w")
+        tab_s = held.tile([P, T], U8, name="tab_s")
+        w2_raw = held.tile([P, 2 * H], U8, name="w2_raw")
+        w2_sraw = held.tile([P, H], U8, name="w2_sraw")
+        w4_w = held.tile([P, 2, 2 * N], U8, name="w4_w", align_bytes=64)
+        w4_s = held.tile([P, 2, N], U8, name="w4_s", align_bytes=64)
+        gains = held.tile([P, 2, PACK], F32, name="gains")
+        pages = [held.tile([P, T2], F32, name="page%d" % s) for s in range(SLICES)]
+        page_rows = page0.rearrange("(a p t) c -> a t p c", a=2, t=PACK)
+
+        nc.vector.memset(tab_s[:].bitcast(I32), 0)
+        nc.vector.memset(w2_sraw[:].bitcast(I32), 0)
+        nc.vector.memset(w4_s[:].rearrange("p a n -> p (a n)").bitcast(I32), 0)
+
+        def load_weight(rows):
+            raw = ring.tile([P, PACK, KP], F32, name="w_raw", tag="w_raw", bufs=3)
+            nc.sync.dma_start(out=raw[:], in_=rows.rearrange("(p j) c -> p j c", j=PACK))
+            return raw
+
+        def load_page(s):
+            nc.sync.dma_start(out=pages[s][:], in_=page_rows[s // PACK, s % PACK])
+
+        nc.sync.dma_start(list1[:], offs)
+        nc.sync.dma_start(list2[:], offs2)
+        nc.sync.dma_start(list3[:], offs3)
+        nc.sync.dma_start(out=w2_raw[:].bitcast(I32), in_=w2_words[0].bitcast(I32))
+        tab_rows = tab_words[0].rearrange("p n t -> p (n t)").bitcast(I32)
+        for part in range(4):
+            cols = slice(part * T // 4, (part + 1) * T // 4)
+            nc.sync.dma_start(out=tab_w[:, cols], in_=tab_rows[:, cols])
+        load_scale_rows(nc.scalar, tab_s, lambda q: tab_scales[0, 4 * q : 4 * q + 4, :])
+        w1_raw = [load_weight(w1[:, 0:KP])]
+        load_page(0)
+        load_scale_rows(nc.scalar, w2_sraw, lambda q: w2_scales[0, 4 * q : 4 * q + 4, :])
+        nc.sync.dma_start(out=gains[:], in_=gain.rearrange("(a p t) -> p a t", a=2, t=PACK))
+        load_page(1)
+        load_page(2)
+        w1_raw.append(load_weight(w1[:, KP : 2 * KP]))
+        for s in range(3, SLICES):
+            load_page(s)
+
+        v_s = held.tile([P, S], U8, name="v_s", align_bytes=64)
+        v_w = held.tile([P, S], U32, name="v_w", align_bytes=64)
+
+        w2_w = held.tile([P, 2 * H], U8, name="w2_w", align_bytes=64)
+        w2_s = held.tile([P, H], U8, name="w2_s", align_bytes=64)
+        nc.vector.tensor_copy(
+            out=w2_w[:].bitcast(U16).rearrange("p (a t m) -> p a t m", a=2, t=PACK),
+            in_=w2_raw[:].bitcast(U16).rearrange("p (a m t) -> p a t m", a=2, t=PACK),
+        )
+
+        def pick_reports(half):
+            cols = slice(half * BANK, (half + 1) * BANK)
+            picks = list1[:, half * BANK // PER_COL : (half + 1) * BANK // PER_COL]
+            nc.vector.tensor_copy(v_s[:, cols], tab_s[:].indirect(picks))
+            nc.vector.tensor_copy(v_w[:, cols], tab_w[:].bitcast(U32).indirect(picks))
+
+        w1_c = [held.tile([P, P], U32, name="w1_c%d" % s, align_bytes=64) for s in range(SLICES)]
+        w1_s = [held.tile([P, P], U8, name="w1_s%d" % s, align_bytes=64) for s in range(SLICES)]
+
+        def quantise_w1(s):
+            a, t = divmod(s, PACK)
+            grouped = ring.tile([P, P, PACK], BF16, name="w1_bf", tag="w1_bf", align_bytes=64)
+            nc.scalar.copy(out=grouped[:], in_=w1_raw[a][:].rearrange("p j (m t) -> p t m j", t=PACK)[:, t])
+            nc.vector.quantize_mx(
+                out=w1_c[s][:].bitcast(FP8X4), scales=w1_s[s][:], in_=grouped[:].rearrange("p m j -> p (m j)")
+            )
+
+        def quantise_weight(rows, name):
+            raw = load_weight(rows)
+            grouped = ring.tile([P, KP, PACK], BF16, name="w_bf", tag="w_bf", align_bytes=64)
+            nc.scalar.copy(out=grouped[:], in_=raw[:].rearrange("p j c -> p c j"))
+            codes = held.tile([P, KP], U32, name=name + "_c", align_bytes=64)
+            scales = held.tile([P, KP], U8, name=name + "_s", align_bytes=64)
+            nc.vector.quantize_mx(
+                out=codes[:].bitcast(FP8X4), scales=scales[:], in_=grouped[:].rearrange("p c j -> p (c j)")
+            )
+            return codes, scales
+
+        def first_stage(s):
+            a, t = divmod(s, PACK)
+            h1 = ring.tile([P, S], F32, name="h1", tag="h1")
+            h2 = ring.tile([P, S], F32, name="h2", tag="h2")
+            for half in range(2):
+                cols = slice(half * BANK, (half + 1) * BANK)
+                acc = bank(half)
+                nc.tensor.matmul_mx(
+                    out=acc[:], lhsT=w1_c[s][:].bitcast(FP8X4), lhsT_scale=w1_s[s][:],
+                    rhs=v_w[:, cols].bitcast(FP8X4), rhs_scale=v_s[:, cols], start=True, stop=True,
+                )
+                nc.scalar.copy(out=h1[:, cols], in_=acc[:])
+            for half in range(2):
+                cols = slice(half * BANK, (half + 1) * BANK)
+                acc = bank(2 + half)
+                nc.tensor.matmul_mx(
+                    out=acc[:], lhsT=w2_w[:, 2 * P * s : 2 * P * (s + 1)].bitcast(FP4X4),
+                    lhsT_scale=w2_s[:, P * s : P * (s + 1)],
+                    rhs=v_w[:, cols].bitcast(FP8X4), rhs_scale=v_s[:, cols], start=True, stop=True,
+                )
+                nc.scalar.activation(out=h2[:, cols], in_=acc[:], func=COPY, scale=gains[:, a, t : t + 1])
+            return h1, h2
+
+        def fetch_and_add(s, h1):
+            state = ring.tile([P, S], F32, name="state", tag="state")
+            nc.vector.tensor_tensor(state[:], pages[s][:].indirect(list2[:]), h1[:], ADD)
+            return state
+
+        def keep_larger(state, h2):
+            nc.vector.tensor_tensor(state[:], state[:], h2[:], MAX)
+
+        def put_back(s, state):
+            nc.vector.tensor_copy(pages[s][:].indirect(list2[:]), state[:])
+
+        x_c = [[held.tile([P, CHUNK], U32, name="x_c%d_%d" % (a, c), tag="x_c%d_%d" % (a, c), align_bytes=64) for c in range(CHUNKS)] for a in range(2)]
+        x_s = [[held.tile([P, CHUNK], U8, name="x_s%d_%d" % (a, c), align_bytes=64) for c in range(CHUNKS)] for a in range(2)]
+
+        def quantise_x(a, c, planes):
+            if a == 1 and c >= 2:
+                grouped = held.tile([P, CHUNK, PACK], BF16, name="x_bf", tag="x_c1_%d" % (c - 2), align_bytes=64)
+            else:
+                grouped = ring.tile([P, CHUNK, PACK], BF16, name="x_bf", tag="x_bf", align_bytes=64)
+            nc.scalar.copy(out=grouped[:], in_=planes.rearrange("p t c -> p c t"))
+            nc.vector.quantize_mx(
+                out=x_c[a][c][:].bitcast(FP8X4), scales=x_s[a][c][:], in_=grouped[:].rearrange("p c t -> p (c t)")
+            )
+
+        read0 = held.tile([P, PACK, S], BF16, name="read0")
+
+        pick_reports(0)
+        quantise_w1(0)
+        pick_reports(1)
+        nc.vector.tensor_copy(
+            out=w2_s[:].rearrange("p (a t m) -> p a t m", a=2, t=PACK),
+            in_=w2_sraw[:].rearrange("p (a m t) -> p a t m", a=2, t=PACK),
+        )
+        h = first_stage(0)
+        quantise_w1(1)
+        state = fetch_and_add(0, h[0])
+        keep_larger(state, h[1])
+        weights = {}
+        for s in range(SLICES):
+            if s + 1 < SLICES:
+                h = first_stage(s + 1)
+                if s + 2 < SLICES:
+                    quantise_w1(s + 2)
+                ahead = fetch_and_add(s + 1, h[0])
+            put_back(s, state)
+            if s + 1 < SLICES:
+                keep_larger(ahead, h[1])
+                state = ahead
+            if s < PACK:
+                nc.vector.tensor_copy(read0[:, s, :], pages[s][:].indirect(list3[:]))
+            if s == 2:
+                weights["w5"] = quantise_weight(w5, "w5")
+                nc.sync.dma_start(out=w4_w[:].bitcast(I32), in_=w4_words.rearrange("a p c -> p a c").bitcast(I32))
+                load_scale_rows(nc.sync, w4_s, lambda q: w4_scales[:, 4 * q : 4 * q + 4, :].rearrange("a r c -> r a c"))
+            if s == 3:
+                weights["w3", 0] = quantise_weight(w3[0:KP, :], "w3a")
+            if s == 4:
+                weights["w3", 1] = quantise_weight(w3[KP : 2 * KP, :], "w3b")
+                for c in range(CHUNKS):
+                    quantise_x(0, c, read0[:, :, c * CHUNK : (c + 1) * CHUNK])
+
+        def mm(acc, i, lhs, lhs_s, rhs, rhs_s, start, stop):
+            nc.tensor.matmul_mx(
+                out=acc[:, i * CHUNK : (i + 1) * CHUNK], lhsT=lhs, lhsT_scale=lhs_s,
+                rhs=rhs.bitcast(FP8X4), rhs_scale=rhs_s, start=start, stop=stop,
+            )
+
+        def skip_pass(acc, i, nt, c, start, stop):
+            n = slice(nt * P, (nt + 1) * P)
+            cols = slice(c * CHUNK, (c + 1) * CHUNK)
+            codes, scales = weights["w5"]
+            mm(acc, i, codes[:, n].bitcast(FP8X4), scales[:, n], v_w[:, cols], v_s[:, cols], start, stop)
+
+        def w3_pass(acc, i, nt, c, a, start, stop):
+            n = slice(nt * P, (nt + 1) * P)
+            codes, scales = weights["w3", a]
+            mm(acc, i, codes[:, n].bitcast(FP8X4), scales[:, n], x_c[a][c][:], x_s[a][c][:], start, stop)
+
+        def w4_pass(acc, i, nt, c, a, start, stop):
+            n = slice(nt * P, (nt + 1) * P)
+            lhs = w4_w[:, a, 2 * nt * P : 2 * (nt + 1) * P].bitcast(FP4X4)
+            mm(acc, i, lhs, w4_s[:, a, n], x_c[a][c][:], x_s[a][c][:], start, stop)
+
+        acc = bank(4)
+        for i in range(2):
+            skip_pass(acc, i, i, 0, True, True)
+        skip0 = held.tile([P, BANK], F32, name="skip0")
+        nc.scalar.copy(out=skip0[:], in_=acc[:])
+
+        def open_chunk(c):
+            first = 4 * ((c + 1) % 2)
+            accs = []
+            for pair in range(2):
+                acc_a, acc_b = bank(first + 2 * pair), bank(first + 2 * pair + 1)
+                apart = c == 0 and pair == 0
+                for acc, product in ((acc_b, w4_pass), (acc_a, w3_pass)):
+                    for i in range(2):
+                        if not apart:
+                            skip_pass(acc, i, 2 * pair + i, c, i == 0, False)
+                        product(acc, i, 2 * pair + i, c, 0, apart and i == 0, False)
+                accs.append((acc_a, acc_b))
+            return accs
+
+        def fetch_chunk(c):
+            planes = ring.tile([P, PACK, CHUNK], BF16, name="read1", tag="state")
+            picks = list3[:, c * CHUNK // PER_COL : (c + 1) * CHUNK // PER_COL]
+            for t in range(PACK):
+                nc.vector.tensor_copy(planes[:, t, :], pages[PACK + t][:].indirect(picks))
+            return planes
+
+        def close_chunk(c, accs):
+            sums = []
+            for pair in range(2):
+                acc_a, acc_b = accs[pair]
+                for acc, product in ((acc_b, w4_pass), (acc_a, w3_pass)):
+                    for i in range(2):
+                        product(acc, i, 2 * pair + i, c, 1, False, i == 1)
+                y_b = ring.tile([P, BANK], F32, name="y_b", tag="y_b", bufs=6)
+                nc.scalar.copy(out=y_b[:], in_=acc_b[:])
+                y_a = acc_a
+                if c < 2:
+                    y_a = ring.tile([P, BANK], F32, name="y_a", tag="y_a", bufs=4)
+                    nc.scalar.copy(out=y_a[:], in_=acc_a[:])
+                sums.append((y_a, y_b))
+            return sums
+
+        def finish(c, pair, y_a, y_b):
+            if c == 0 and pair == 0:
+                result = held.tile([P, BANK], F32, name="result", tag="x_c1_0", align_bytes=64)
+            else:
+                result = ring.tile([P, BANK], F32, name="result", tag="result", bufs=4)
+            nc.vector.tensor_tensor(result[:], y_a[:], y_b[:], MAX)
+            if c == 0 and pair == 0:
+                nc.vector.tensor_tensor(result[:], result[:], skip0[:], ADD)
+            rows = out[2 * pair * P : 2 * (pair + 1) * P, c * CHUNK : (c + 1) * CHUNK]
+            nc.sync.dma_start(
+                out=rows.rearrange("(i p) c -> p i c", i=2), in_=result[:].rearrange("p (i c) -> p i c", i=2)
+            )
+
+        accs = {0: open_chunk(0), 1: open_chunk(1)}
+        planes = {0: fetch_chunk(0), 1: fetch_chunk(1)}
+        sums = {}
+        for c in range(CHUNKS):
+            quantise_x(1, c, planes[c][:])
+            if c + 2 < CHUNKS:
+                planes[c + 2] = fetch_chunk(c + 2)
+            else:
+                for pair in range(2):
+                    finish(c - 2, pair, *sums[c - 2][pair])
+            sums[c] = close_chunk(c, accs[c])
+            if c + 2 < CHUNKS:
+                accs[c + 2] = open_chunk(c + 2)
+        for c in range(CHUNKS - 2, CHUNKS):
+            for pair in range(2):
+                finish(c, pair, *sums[c][pair])

@@ -22,9 +22,13 @@ PACK = 4
 KP = P * PACK
 BANK = 512
 SLICES = H // P
+PER_COL = 16
+MX_ALIGN = 64
 CHUNK = 256
 CHUNKS = S // CHUNK
-PER_COL = 16
+TABLE_LOADS = 4
+STATES = 3
+ADDED_AFTER = (2, 0)
 
 
 def tile_list_building_tag_features_kernel(
@@ -40,225 +44,259 @@ def tile_list_building_tag_features_kernel(
         def bank(b):
             return psum.tile([P, BANK], F32, name="bank%d" % b, tag="bank%d" % b)
 
-        def load_scale_rows(queue, plane, rows):
-            for q in range(4):
-                queue.dma_start(out=plane[32 * q : 32 * q + 4].bitcast(I32), in_=rows(q).bitcast(I32))
+        def entries(offsets, cols):
+            return offsets[:, cols.start // PER_COL : cols.stop // PER_COL]
+
+        def operand(name, columns, tag=""):
+            words = held.tile([P, columns], U32, name=name + "_words", tag=tag, align_bytes=MX_ALIGN)
+            scales = held.tile([P, columns], U8, name=name + "_scales", align_bytes=MX_ALIGN)
+            return words, scales
+
+        def quantise(target, woven):
+            words, scales = target
+            nc.vector.quantize_mx(out=words.bitcast(FP8X4), scales=scales, in_=woven)
 
         list1 = lists.tile([P, S // PER_COL], U16, name="list1")
         list2 = lists.tile([P, S // PER_COL], U16, name="list2")
         list3 = lists.tile([P, S // PER_COL], U16, name="list3")
-
-        tab_w = held.tile([P, T], I32, name="tab_w")
-        tab_s = held.tile([P, T], U8, name="tab_s")
-        w2_raw = held.tile([P, 2 * H], U8, name="w2_raw")
-        w2_sraw = held.tile([P, H], U8, name="w2_sraw")
-        w4_w = held.tile([P, 2, 2 * N], U8, name="w4_w", align_bytes=64)
-        w4_s = held.tile([P, 2, N], U8, name="w4_s", align_bytes=64)
+        table_words = held.tile([P, T], I32, name="table_words", tag="table_words")
+        table_scales = held.tile([P, T], U8, name="table_scales")
+        w2_words_in = held.tile([P, 2 * H], U8, name="w2_words_in")
+        w2_scales_in = held.tile([P, H], U8, name="w2_scales_in")
+        w4_word_tile = held.tile([P, 2, 2 * N], U8, name="w4_word_tile", align_bytes=MX_ALIGN)
+        w4_scale_tile = held.tile([P, 2, N], U8, name="w4_scale_tile", align_bytes=MX_ALIGN)
         gains = held.tile([P, 2, PACK], F32, name="gains")
         pages = [held.tile([P, T2], F32, name="page%d" % s) for s in range(SLICES)]
         page_rows = page0.rearrange("(a p t) c -> a t p c", a=2, t=PACK)
 
-        nc.vector.memset(tab_s[:].bitcast(I32), 0)
-        nc.vector.memset(w2_sraw[:].bitcast(I32), 0)
-        nc.vector.memset(w4_s[:].rearrange("p a n -> p (a n)").bitcast(I32), 0)
+        nc.vector.memset(table_scales[:].bitcast(I32), 0)
+        nc.vector.memset(w2_scales_in[:].bitcast(I32), 0)
+        nc.vector.memset(w4_scale_tile[:].rearrange("p a n -> p (a n)").bitcast(I32), 0)
 
-        def load_weight(rows):
-            raw = ring.tile([P, PACK, KP], F32, name="w_raw", tag="w_raw", bufs=3)
-            nc.sync.dma_start(out=raw[:], in_=rows.rearrange("(p j) c -> p j c", j=PACK))
-            return raw
+        def load_scale_rows(queue, tile, rows):
+            for q in range(4):
+                queue.dma_start(out=tile[32 * q : 32 * q + 4].bitcast(I32), in_=rows(slice(4 * q, 4 * q + 4)).bitcast(I32))
+
+        def load_rows(tile, rows):
+            nc.sync.dma_start(out=tile, in_=rows.rearrange("(p j) c -> p j c", j=PACK))
 
         def load_page(s):
             nc.sync.dma_start(out=pages[s][:], in_=page_rows[s // PACK, s % PACK])
 
+        w1_in = [held.tile([P, PACK, KP], F32, name="w1_in%d" % a) for a in range(2)]
+        w5_in = held.tile([P, PACK, N], F32, name="w5_in")
+
         nc.sync.dma_start(list1[:], offs)
         nc.sync.dma_start(list2[:], offs2)
         nc.sync.dma_start(list3[:], offs3)
-        nc.sync.dma_start(out=w2_raw[:].bitcast(I32), in_=w2_words[0].bitcast(I32))
-        tab_rows = tab_words[0].rearrange("p n t -> p (n t)").bitcast(I32)
-        for part in range(4):
-            cols = slice(part * T // 4, (part + 1) * T // 4)
-            nc.sync.dma_start(out=tab_w[:, cols], in_=tab_rows[:, cols])
-        load_scale_rows(nc.scalar, tab_s, lambda q: tab_scales[0, 4 * q : 4 * q + 4, :])
-        w1_raw = [load_weight(w1[:, 0:KP])]
+        nc.sync.dma_start(out=w2_words_in[:].bitcast(I32), in_=w2_words[0].bitcast(I32))
+        table_rows = tab_words[0].rearrange("p n t -> p (n t)").bitcast(I32)
+        for part in range(TABLE_LOADS):
+            cols = slice(part * T // TABLE_LOADS, (part + 1) * T // TABLE_LOADS)
+            nc.sync.dma_start(out=table_words[:, cols], in_=table_rows[:, cols])
+        load_scale_rows(nc.scalar, table_scales, lambda rows: tab_scales[0, rows, :])
+        load_rows(w1_in[0][:], w1[:, 0:KP])
         load_page(0)
-        load_scale_rows(nc.scalar, w2_sraw, lambda q: w2_scales[0, 4 * q : 4 * q + 4, :])
+        load_scale_rows(nc.scalar, w2_scales_in, lambda rows: w2_scales[0, rows, :])
         nc.sync.dma_start(out=gains[:], in_=gain.rearrange("(a p t) -> p a t", a=2, t=PACK))
         load_page(1)
         load_page(2)
-        w1_raw.append(load_weight(w1[:, KP : 2 * KP]))
-        for s in range(3, SLICES):
+        load_rows(w1_in[1][:], w1[:, KP : 2 * KP])
+        load_page(3)
+        load_rows(w5_in[:], w5)
+        nc.sync.dma_start(out=w4_word_tile[:].bitcast(I32), in_=w4_words.rearrange("a p c -> p a c").bitcast(I32))
+        load_scale_rows(nc.sync, w4_scale_tile, lambda rows: w4_scales[:, rows, :].rearrange("a r c -> r a c"))
+        for s in range(PACK, SLICES):
             load_page(s)
 
-        v_s = held.tile([P, S], U8, name="v_s", align_bytes=64)
-        v_w = held.tile([P, S], U32, name="v_w", align_bytes=64)
+        v_words, v_scales = operand("v", S)
+        w2_word_tile = held.tile([P, 2 * H], U8, name="w2_word_tile", align_bytes=MX_ALIGN)
+        w2_scale_tile = held.tile([P, H], U8, name="w2_scale_tile", align_bytes=MX_ALIGN)
+        w1_mx = [operand("w1_%d" % a, KP) for a in range(2)]
 
-        w2_w = held.tile([P, 2 * H], U8, name="w2_w", align_bytes=64)
-        w2_s = held.tile([P, H], U8, name="w2_s", align_bytes=64)
-        nc.vector.tensor_copy(
-            out=w2_w[:].bitcast(U16).rearrange("p (a t m) -> p a t m", a=2, t=PACK),
-            in_=w2_raw[:].bitcast(U16).rearrange("p (a m t) -> p a t m", a=2, t=PACK),
-        )
+        def deal_w2(dealt, loaded):
+            nc.vector.tensor_copy(
+                out=dealt.rearrange("p (a t m) -> p a t m", a=2, t=PACK),
+                in_=loaded.rearrange("p (a m t) -> p a t m", a=2, t=PACK),
+            )
 
         def pick_reports(half):
             cols = slice(half * BANK, (half + 1) * BANK)
-            picks = list1[:, half * BANK // PER_COL : (half + 1) * BANK // PER_COL]
-            nc.vector.tensor_copy(v_s[:, cols], tab_s[:].indirect(picks))
-            nc.vector.tensor_copy(v_w[:, cols], tab_w[:].bitcast(U32).indirect(picks))
+            nc.vector.tensor_copy(v_scales[:, cols], table_scales[:].indirect(entries(list1, cols)))
+            nc.vector.tensor_copy(v_words[:, cols], table_words[:].bitcast(U32).indirect(entries(list1, cols)))
 
-        w1_c = [held.tile([P, P], U32, name="w1_c%d" % s, align_bytes=64) for s in range(SLICES)]
-        w1_s = [held.tile([P, P], U8, name="w1_s%d" % s, align_bytes=64) for s in range(SLICES)]
+        def dealt_w1(a):
+            return w1_in[a][:].rearrange("p j (m t) -> p t m j", t=PACK)
 
-        def quantise_w1(s):
+        def quantise_w1_slice(t):
+            woven = ring.tile([P, P, PACK], BF16, name="w1_woven", align_bytes=MX_ALIGN, bufs=PACK)
+            nc.scalar.copy(out=woven[:], in_=dealt_w1(0)[:, t])
+            cols = slice(t * P, (t + 1) * P)
+            quantise((w1_mx[0][0][:, cols], w1_mx[0][1][:, cols]), woven[:].rearrange("p m j -> p (m j)"))
+
+        deal_w2(w2_word_tile[:].bitcast(U16), w2_words_in[:].bitcast(U16))
+        pick_reports(0)
+        quantise_w1_slice(0)
+        pick_reports(1)
+        deal_w2(w2_scale_tile[:], w2_scales_in[:])
+
+        w3_in = held.tile([P, 2, PACK, N], F32, name="w3_in", tag="table_words")
+        for a in range(2):
+            load_rows(w3_in[:, a], w3[a * KP : (a + 1) * KP, :])
+
+        def products(s):
             a, t = divmod(s, PACK)
-            grouped = ring.tile([P, P, PACK], BF16, name="w1_bf", tag="w1_bf", align_bytes=64)
-            nc.scalar.copy(out=grouped[:], in_=w1_raw[a][:].rearrange("p j (m t) -> p t m j", t=PACK)[:, t])
-            nc.vector.quantize_mx(
-                out=w1_c[s][:].bitcast(FP8X4), scales=w1_s[s][:], in_=grouped[:].rearrange("p m j -> p (m j)")
-            )
-
-        def quantise_weight(rows, name):
-            raw = load_weight(rows)
-            grouped = ring.tile([P, KP, PACK], BF16, name="w_bf", tag="w_bf", align_bytes=64)
-            nc.scalar.copy(out=grouped[:], in_=raw[:].rearrange("p j c -> p c j"))
-            codes = held.tile([P, KP], U32, name=name + "_c", align_bytes=64)
-            scales = held.tile([P, KP], U8, name=name + "_s", align_bytes=64)
-            nc.vector.quantize_mx(
-                out=codes[:].bitcast(FP8X4), scales=scales[:], in_=grouped[:].rearrange("p c j -> p (c j)")
-            )
-            return codes, scales
-
-        def first_stage(s):
-            a, t = divmod(s, PACK)
-            h1 = ring.tile([P, S], F32, name="h1", tag="h1")
-            h2 = ring.tile([P, S], F32, name="h2", tag="h2")
+            cols_r = slice(t * P, (t + 1) * P)
+            h1 = ring.tile([P, S], F32, name="h1")
+            level = ring.tile([P, S], F32, name="level")
             for half in range(2):
                 cols = slice(half * BANK, (half + 1) * BANK)
                 acc = bank(half)
                 nc.tensor.matmul_mx(
-                    out=acc[:], lhsT=w1_c[s][:].bitcast(FP8X4), lhsT_scale=w1_s[s][:],
-                    rhs=v_w[:, cols].bitcast(FP8X4), rhs_scale=v_s[:, cols], start=True, stop=True,
+                    out=acc[:],
+                    lhsT=w1_mx[a][0][:, cols_r].bitcast(FP8X4),
+                    lhsT_scale=w1_mx[a][1][:, cols_r],
+                    rhs=v_words[:, cols].bitcast(FP8X4),
+                    rhs_scale=v_scales[:, cols],
+                    start=True,
+                    stop=True,
                 )
                 nc.scalar.copy(out=h1[:, cols], in_=acc[:])
             for half in range(2):
                 cols = slice(half * BANK, (half + 1) * BANK)
                 acc = bank(2 + half)
                 nc.tensor.matmul_mx(
-                    out=acc[:], lhsT=w2_w[:, 2 * P * s : 2 * P * (s + 1)].bitcast(FP4X4),
-                    lhsT_scale=w2_s[:, P * s : P * (s + 1)],
-                    rhs=v_w[:, cols].bitcast(FP8X4), rhs_scale=v_s[:, cols], start=True, stop=True,
+                    out=acc[:],
+                    lhsT=w2_word_tile[:, 2 * P * s : 2 * P * (s + 1)].bitcast(FP4X4),
+                    lhsT_scale=w2_scale_tile[:, P * s : P * (s + 1)],
+                    rhs=v_words[:, cols].bitcast(FP8X4),
+                    rhs_scale=v_scales[:, cols],
+                    start=True,
+                    stop=True,
                 )
-                nc.scalar.activation(out=h2[:, cols], in_=acc[:], func=COPY, scale=gains[:, a, t : t + 1])
-            return h1, h2
+                nc.scalar.activation(out=level[:, cols], in_=acc[:], func=COPY, scale=gains[:, a, t : t + 1])
+            return h1, level
+
+        states = [held.tile([P, S], F32, name="state%d" % i, align_bytes=MX_ALIGN) for i in range(STATES)]
 
         def fetch_and_add(s, h1):
-            state = ring.tile([P, S], F32, name="state", tag="state")
-            nc.vector.tensor_tensor(state[:], pages[s][:].indirect(list2[:]), h1[:], ADD)
-            return state
+            pieces = 2 if s == 0 else 1
+            for i in range(pieces):
+                cols = slice(i * S // pieces, (i + 1) * S // pieces)
+                nc.vector.tensor_tensor(
+                    states[s % STATES][:, cols], pages[s][:].indirect(entries(list2, cols)), h1[:, cols], ADD
+                )
 
-        def keep_larger(state, h2):
-            nc.vector.tensor_tensor(state[:], state[:], h2[:], MAX)
+        def keep_larger(s, level):
+            state = states[s % STATES]
+            nc.vector.tensor_tensor(state[:], state[:], level[:], MAX)
 
-        def put_back(s, state):
-            nc.vector.tensor_copy(pages[s][:].indirect(list2[:]), state[:])
+        def put_back(s):
+            nc.vector.tensor_copy(pages[s][:].indirect(list2[:]), states[s % STATES][:])
 
-        x_c = [[held.tile([P, CHUNK], U32, name="x_c%d_%d" % (a, c), tag="x_c%d_%d" % (a, c), align_bytes=64) for c in range(CHUNKS)] for a in range(2)]
-        x_s = [[held.tile([P, CHUNK], U8, name="x_s%d_%d" % (a, c), align_bytes=64) for c in range(CHUNKS)] for a in range(2)]
+        w5_mx = operand("w5", N)
+        w3_mx = [operand("w3_%d" % a, N) for a in range(2)]
+        staged = [
+            (w1_mx[1], dealt_w1(1), "p (t m j) -> p t m j", {"t": PACK, "j": PACK}),
+            (w5_mx, w5_in[:].rearrange("p j c -> p c j"), "p (c j) -> p c j", {"j": PACK}),
+            (w3_mx[0], w3_in[:, 0].rearrange("p j c -> p c j"), "p (c j) -> p c j", {"j": PACK}),
+            (w3_mx[1], w3_in[:, 1].rearrange("p j c -> p c j"), "p (c j) -> p c j", {"j": PACK}),
+        ]
 
-        def quantise_x(a, c, planes):
-            if a == 1 and c >= 2:
-                grouped = held.tile([P, CHUNK, PACK], BF16, name="x_bf", tag="x_c1_%d" % (c - 2), align_bytes=64)
-            else:
-                grouped = ring.tile([P, CHUNK, PACK], BF16, name="x_bf", tag="x_bf", align_bytes=64)
-            nc.scalar.copy(out=grouped[:], in_=planes.rearrange("p t c -> p c t"))
-            nc.vector.quantize_mx(
-                out=x_c[a][c][:].bitcast(FP8X4), scales=x_s[a][c][:], in_=grouped[:].rearrange("p c t -> p (c t)")
-            )
+        def quantise_staged(s):
+            (words, scales), source, view, sizes = staged[s]
+            woven = states[s % STATES][:].bitcast(BF16)
+            nc.scalar.copy(out=woven.rearrange(view, **sizes), in_=source)
+            quantise((words[:], scales[:]), woven)
 
-        read0 = held.tile([P, PACK, S], BF16, name="read0")
+        x_mx = [
+            [operand("x%d_%d" % (a, c), CHUNK, tag="x%d_%d" % (a, c)) for c in range(CHUNKS)] for a in range(2)
+        ]
+        planes_pass0 = held.tile([P, PACK, S], BF16, name="planes_pass0")
 
-        pick_reports(0)
-        quantise_w1(0)
-        pick_reports(1)
-        nc.vector.tensor_copy(
-            out=w2_s[:].rearrange("p (a t m) -> p a t m", a=2, t=PACK),
-            in_=w2_sraw[:].rearrange("p (a m t) -> p a t m", a=2, t=PACK),
-        )
-        h = first_stage(0)
-        quantise_w1(1)
-        state = fetch_and_add(0, h[0])
-        keep_larger(state, h[1])
-        weights = {}
+        def as_planes(tile):
+            return tile[:].bitcast(BF16)[:, 0 : PACK * CHUNK].rearrange("p (t c) -> p t c", t=PACK)
+
+        def fetch_planes(planes, c, which):
+            cols = slice(c * CHUNK, (c + 1) * CHUNK)
+            for t in which:
+                nc.vector.tensor_copy(planes[:, t, :], pages[PACK + t][:].indirect(entries(list3, cols)))
+
+        def quantise_x(a, c, planes, tile):
+            woven = tile[:].bitcast(BF16)
+            nc.scalar.copy(out=woven.rearrange("p (c t) -> p c t", t=PACK), in_=planes.rearrange("p t c -> p c t"))
+            quantise((x_mx[a][c][0][:], x_mx[a][c][1][:]), woven)
+
+        h1, level = products(0)
+        for t in range(1, PACK):
+            quantise_w1_slice(t)
+        fetch_and_add(0, h1)
+        keep_larger(0, level)
+        planes = {}
         for s in range(SLICES):
             if s + 1 < SLICES:
-                h = first_stage(s + 1)
-                if s + 2 < SLICES:
-                    quantise_w1(s + 2)
-                ahead = fetch_and_add(s + 1, h[0])
-            put_back(s, state)
+                h1, level = products(s + 1)
+                fetch_and_add(s + 1, h1)
+            put_back(s)
             if s + 1 < SLICES:
-                keep_larger(ahead, h[1])
-                state = ahead
+                keep_larger(s + 1, level)
             if s < PACK:
-                nc.vector.tensor_copy(read0[:, s, :], pages[s][:].indirect(list3[:]))
-            if s == 2:
-                weights["w5"] = quantise_weight(w5, "w5")
-                nc.sync.dma_start(out=w4_w[:].bitcast(I32), in_=w4_words.rearrange("a p c -> p a c").bitcast(I32))
-                load_scale_rows(nc.sync, w4_s, lambda q: w4_scales[:, 4 * q : 4 * q + 4, :].rearrange("a r c -> r a c"))
-            if s == 3:
-                weights["w3", 0] = quantise_weight(w3[0:KP, :], "w3a")
-            if s == 4:
-                weights["w3", 1] = quantise_weight(w3[KP : 2 * KP, :], "w3b")
+                nc.vector.tensor_copy(planes_pass0[:, s, :], pages[s][:].indirect(list3[:]))
+                quantise_staged(s)
+            if s == PACK:
                 for c in range(CHUNKS):
-                    quantise_x(0, c, read0[:, :, c * CHUNK : (c + 1) * CHUNK])
+                    tile = ring.tile([P, 2 * CHUNK], U32, name="x0_woven", align_bytes=MX_ALIGN, bufs=CHUNKS)
+                    quantise_x(0, c, planes_pass0[:, :, c * CHUNK : (c + 1) * CHUNK], tile)
+            if s == SLICES - 2:
+                planes[0] = as_planes(states[s % STATES])
+                fetch_planes(planes[0], 0, range(PACK - 1))
 
-        def mm(acc, i, lhs, lhs_s, rhs, rhs_s, start, stop):
+        def mx_pass(acc, i, lhs_words, lhs_scales, rhs_words, rhs_scales, start, stop):
             nc.tensor.matmul_mx(
-                out=acc[:, i * CHUNK : (i + 1) * CHUNK], lhsT=lhs, lhsT_scale=lhs_s,
-                rhs=rhs.bitcast(FP8X4), rhs_scale=rhs_s, start=start, stop=stop,
+                out=acc[:, i * CHUNK : (i + 1) * CHUNK],
+                lhsT=lhs_words,
+                lhsT_scale=lhs_scales,
+                rhs=rhs_words.bitcast(FP8X4),
+                rhs_scale=rhs_scales,
+                start=start,
+                stop=stop,
             )
 
-        def skip_pass(acc, i, nt, c, start, stop):
-            n = slice(nt * P, (nt + 1) * P)
+        def w5_pass(acc, i, c, pair, start, stop):
+            n = slice((2 * pair + i) * P, (2 * pair + i + 1) * P)
             cols = slice(c * CHUNK, (c + 1) * CHUNK)
-            codes, scales = weights["w5"]
-            mm(acc, i, codes[:, n].bitcast(FP8X4), scales[:, n], v_w[:, cols], v_s[:, cols], start, stop)
+            mx_pass(acc, i, w5_mx[0][:, n].bitcast(FP8X4), w5_mx[1][:, n], v_words[:, cols], v_scales[:, cols], start, stop)
 
-        def w3_pass(acc, i, nt, c, a, start, stop):
-            n = slice(nt * P, (nt + 1) * P)
-            codes, scales = weights["w3", a]
-            mm(acc, i, codes[:, n].bitcast(FP8X4), scales[:, n], x_c[a][c][:], x_s[a][c][:], start, stop)
+        def w3_pass(acc, i, c, pair, a, start, stop):
+            n = slice((2 * pair + i) * P, (2 * pair + i + 1) * P)
+            words, scales = x_mx[a][c]
+            mx_pass(acc, i, w3_mx[a][0][:, n].bitcast(FP8X4), w3_mx[a][1][:, n], words[:], scales[:], start, stop)
 
-        def w4_pass(acc, i, nt, c, a, start, stop):
-            n = slice(nt * P, (nt + 1) * P)
-            lhs = w4_w[:, a, 2 * nt * P : 2 * (nt + 1) * P].bitcast(FP4X4)
-            mm(acc, i, lhs, w4_s[:, a, n], x_c[a][c][:], x_s[a][c][:], start, stop)
+        def w4_pass(acc, i, c, pair, a, start, stop):
+            n = slice((2 * pair + i) * P, (2 * pair + i + 1) * P)
+            words, scales = x_mx[a][c]
+            lhs = w4_word_tile[:, a, 2 * n.start : 2 * n.stop].bitcast(FP4X4)
+            mx_pass(acc, i, lhs, w4_scale_tile[:, a, n], words[:], scales[:], start, stop)
 
         acc = bank(4)
         for i in range(2):
-            skip_pass(acc, i, i, 0, True, True)
-        skip0 = held.tile([P, BANK], F32, name="skip0")
-        nc.scalar.copy(out=skip0[:], in_=acc[:])
+            w5_pass(acc, i, *ADDED_AFTER, True, True)
+        skip = held.tile([P, BANK], F32, name="skip")
+        nc.scalar.copy(out=skip[:], in_=acc[:])
 
         def open_chunk(c):
             first = 4 * ((c + 1) % 2)
             accs = []
             for pair in range(2):
                 acc_a, acc_b = bank(first + 2 * pair), bank(first + 2 * pair + 1)
-                apart = c == 0 and pair == 0
+                inside = (c, pair) != ADDED_AFTER
                 for acc, product in ((acc_b, w4_pass), (acc_a, w3_pass)):
                     for i in range(2):
-                        if not apart:
-                            skip_pass(acc, i, 2 * pair + i, c, i == 0, False)
-                        product(acc, i, 2 * pair + i, c, 0, apart and i == 0, False)
+                        if inside:
+                            w5_pass(acc, i, c, pair, i == 0, False)
+                        product(acc, i, c, pair, 0, i == 0 and not inside, False)
                 accs.append((acc_a, acc_b))
             return accs
-
-        def fetch_chunk(c):
-            planes = ring.tile([P, PACK, CHUNK], BF16, name="read1", tag="state")
-            picks = list3[:, c * CHUNK // PER_COL : (c + 1) * CHUNK // PER_COL]
-            for t in range(PACK):
-                nc.vector.tensor_copy(planes[:, t, :], pages[PACK + t][:].indirect(picks))
-            return planes
 
         def close_chunk(c, accs):
             sums = []
@@ -266,42 +304,52 @@ def tile_list_building_tag_features_kernel(
                 acc_a, acc_b = accs[pair]
                 for acc, product in ((acc_b, w4_pass), (acc_a, w3_pass)):
                     for i in range(2):
-                        product(acc, i, 2 * pair + i, c, 1, False, i == 1)
-                y_b = ring.tile([P, BANK], F32, name="y_b", tag="y_b", bufs=6)
+                        product(acc, i, c, pair, 1, False, i == 1)
+                y_b = ring.tile([P, BANK], F32, name="y_b", bufs=4)
                 nc.scalar.copy(out=y_b[:], in_=acc_b[:])
                 y_a = acc_a
                 if c < 2:
-                    y_a = ring.tile([P, BANK], F32, name="y_a", tag="y_a", bufs=4)
+                    y_a = ring.tile([P, BANK], F32, name="y_a", bufs=4)
                     nc.scalar.copy(out=y_a[:], in_=acc_a[:])
                 sums.append((y_a, y_b))
             return sums
 
-        def finish(c, pair, y_a, y_b):
-            if c == 0 and pair == 0:
-                result = held.tile([P, BANK], F32, name="result", tag="x_c1_0", align_bytes=64)
-            else:
-                result = ring.tile([P, BANK], F32, name="result", tag="result", bufs=4)
-            nc.vector.tensor_tensor(result[:], y_a[:], y_b[:], MAX)
-            if c == 0 and pair == 0:
-                nc.vector.tensor_tensor(result[:], result[:], skip0[:], ADD)
-            rows = out[2 * pair * P : 2 * (pair + 1) * P, c * CHUNK : (c + 1) * CHUNK]
-            nc.sync.dma_start(
-                out=rows.rearrange("(i p) c -> p i c", i=2), in_=result[:].rearrange("p (i c) -> p i c", i=2)
-            )
-
-        accs = {0: open_chunk(0), 1: open_chunk(1)}
-        planes = {0: fetch_chunk(0), 1: fetch_chunk(1)}
-        sums = {}
-        for c in range(CHUNKS):
-            quantise_x(1, c, planes[c][:])
-            if c + 2 < CHUNKS:
-                planes[c + 2] = fetch_chunk(c + 2)
-            else:
-                for pair in range(2):
-                    finish(c - 2, pair, *sums[c - 2][pair])
-            sums[c] = close_chunk(c, accs[c])
-            if c + 2 < CHUNKS:
-                accs[c + 2] = open_chunk(c + 2)
-        for c in range(CHUNKS - 2, CHUNKS):
+        def finish_chunk(c, sums):
             for pair in range(2):
-                finish(c, pair, *sums[c][pair])
+                y_a, y_b = sums[pair]
+                if (c, pair) == (0, 0):
+                    result = held.tile([P, BANK], F32, name="result", tag="x1_0", align_bytes=MX_ALIGN)
+                else:
+                    result = ring.tile([P, BANK], F32, name="result", bufs=4)
+                nc.vector.tensor_tensor(result[:], y_a[:], y_b[:], MAX)
+                if (c, pair) == ADDED_AFTER:
+                    nc.vector.tensor_tensor(result[:], result[:], skip[:], ADD)
+                rows = out[2 * pair * P : 2 * (pair + 1) * P, c * CHUNK : (c + 1) * CHUNK]
+                nc.sync.dma_start(
+                    out=rows.rearrange("(i p) c -> p i c", i=2), in_=result[:].rearrange("p (i c) -> p i c", i=2)
+                )
+
+        woven_x1 = [held.tile([P, 2 * CHUNK], U32, name="x1_woven%d" % c, align_bytes=MX_ALIGN) for c in range(2)]
+        accs = {0: open_chunk(0), 1: open_chunk(1)}
+        fetch_planes(planes[0], 0, [PACK - 1])
+        planes[1] = as_planes(states[(SLICES - 1) % STATES])
+        fetch_planes(planes[1], 1, range(PACK))
+        sums = {}
+
+        def quantise_late(c):
+            tile = held.tile([P, 2 * CHUNK], U32, name="x1_woven", tag="x1_%d" % (c - 2), align_bytes=MX_ALIGN)
+            quantise_x(1, c, planes[c], tile)
+
+        for c in range(2):
+            quantise_x(1, c, planes[c], woven_x1[c])
+            planes[c + 2] = as_planes(woven_x1[c])
+            fetch_planes(planes[c + 2], c + 2, range(PACK))
+            if c == 1:
+                quantise_late(2)
+            sums[c] = close_chunk(c, accs[c])
+            accs[c + 2] = open_chunk(c + 2)
+        quantise_late(3)
+        for c in range(CHUNKS):
+            if c >= 2:
+                sums[c] = close_chunk(c, accs[c])
+            finish_chunk(c, sums[c])

from contextlib import ExitStack

import concourse.mybir as mybir

K, H, N, T, S, T2 = 512, 1024, 512, 4096, 1024, 2048
FLOPS = 2 * S * (2 * K * H + 2 * H * N + K * N)

F32 = mybir.dt.float32
BF16 = mybir.dt.bfloat16
I32 = mybir.dt.int32
U32 = mybir.dt.uint32
U16 = mybir.dt.uint16
U8 = mybir.dt.uint8
FP8X4 = mybir.dt.float8_e4m3fn_x4
FP4X4 = mybir.dt.float4_e2m1fn_x4
ADD = mybir.AluOpType.add
MAX = mybir.AluOpType.max
COPY = mybir.ActivationFunctionType.Copy

P = 128
PACK = 4
KP = P * PACK
BANK = 512
SLICES = H // P
PER_COL = 16
MX_ALIGN = 64
CHUNK = 256
CHUNKS = S // CHUNK
TABLE_LOADS = 4
STATES = 3
ADDED_AFTER = (2, 0)


def tile_list_building_tag_features_kernel(
    tc, tab_words, tab_scales, offs, offs2, offs3, w1, w2_words, w2_scales, gain, page0, w3, w4_words, w4_scales, w5, out
):
    nc = tc.nc
    with ExitStack() as ctx:
        lists = ctx.enter_context(tc.tile_pool(name="lists", bufs=1))
        held = ctx.enter_context(tc.tile_pool(name="held", bufs=1))
        ring = ctx.enter_context(tc.tile_pool(name="ring", bufs=2))
        psum = ctx.enter_context(tc.psum_pool(name="psum", bufs=1))

        def bank(b):
            return psum.tile([P, BANK], F32, name="bank%d" % b, tag="bank%d" % b)

        def entries(offsets, cols):
            return offsets[:, cols.start // PER_COL : cols.stop // PER_COL]

        def operand(name, columns, tag=""):
            words = held.tile([P, columns], U32, name=name + "_words", tag=tag, align_bytes=MX_ALIGN)
            scales = held.tile([P, columns], U8, name=name + "_scales", align_bytes=MX_ALIGN)
            return words, scales

        def quantise(target, woven):
            words, scales = target
            nc.vector.quantize_mx(out=words.bitcast(FP8X4), scales=scales, in_=woven)

        list1 = lists.tile([P, S // PER_COL], U16, name="list1")
        list2 = lists.tile([P, S // PER_COL], U16, name="list2")
        list3 = lists.tile([P, S // PER_COL], U16, name="list3")
        table_words = held.tile([P, T], I32, name="table_words", tag="table_words")
        table_scales = held.tile([P, T], U8, name="table_scales")
        w2_words_in = held.tile([P, 2 * H], U8, name="w2_words_in")
        w2_scales_in = held.tile([P, H], U8, name="w2_scales_in")
        w4_word_tile = held.tile([P, 2, 2 * N], U8, name="w4_word_tile", align_bytes=MX_ALIGN)
        w4_scale_tile = held.tile([P, 2, N], U8, name="w4_scale_tile", align_bytes=MX_ALIGN)
        gains = held.tile([P, 2, PACK], F32, name="gains")
        pages = [held.tile([P, T2], F32, name="page%d" % s) for s in range(SLICES)]
        page_rows = page0.rearrange("(a p t) c -> a t p c", a=2, t=PACK)

        nc.vector.memset(table_scales[:].bitcast(I32), 0)
        nc.vector.memset(w2_scales_in[:].bitcast(I32), 0)
        nc.vector.memset(w4_scale_tile[:].rearrange("p a n -> p (a n)").bitcast(I32), 0)

        def load_scale_rows(queue, tile, rows):
            for q in range(4):
                queue.dma_start(out=tile[32 * q : 32 * q + 4].bitcast(I32), in_=rows(slice(4 * q, 4 * q + 4)).bitcast(I32))

        def load_rows(tile, rows):
            nc.sync.dma_start(out=tile, in_=rows.rearrange("(p j) c -> p j c", j=PACK))

        def load_page(s):
            nc.sync.dma_start(out=pages[s][:], in_=page_rows[s // PACK, s % PACK])

        w1_in = [held.tile([P, PACK, KP], F32, name="w1_in%d" % a) for a in range(2)]
        w5_in = held.tile([P, PACK, N], F32, name="w5_in")

        nc.sync.dma_start(list1[:], offs)
        nc.sync.dma_start(list2[:], offs2)
        nc.sync.dma_start(list3[:], offs3)
        nc.sync.dma_start(out=w2_words_in[:].bitcast(I32), in_=w2_words[0].bitcast(I32))
        table_rows = tab_words[0].rearrange("p n t -> p (n t)").bitcast(I32)
        for part in range(TABLE_LOADS):
            cols = slice(part * T // TABLE_LOADS, (part + 1) * T // TABLE_LOADS)
            nc.sync.dma_start(out=table_words[:, cols], in_=table_rows[:, cols])
        load_scale_rows(nc.scalar, table_scales, lambda rows: tab_scales[0, rows, :])
        load_rows(w1_in[0][:], w1[:, 0:KP])
        load_page(0)
        load_scale_rows(nc.scalar, w2_scales_in, lambda rows: w2_scales[0, rows, :])
        nc.sync.dma_start(out=gains[:], in_=gain.rearrange("(a p t) -> p a t", a=2, t=PACK))
        load_page(1)
        load_page(2)
        load_rows(w1_in[1][:], w1[:, KP : 2 * KP])
        load_page(3)
        load_rows(w5_in[:], w5)
        nc.sync.dma_start(out=w4_word_tile[:].bitcast(I32), in_=w4_words.rearrange("a p c -> p a c").bitcast(I32))
        load_scale_rows(nc.sync, w4_scale_tile, lambda rows: w4_scales[:, rows, :].rearrange("a r c -> r a c"))
        for s in range(PACK, SLICES):
            load_page(s)

        v_words, v_scales = operand("v", S)
        w2_word_tile = held.tile([P, 2 * H], U8, name="w2_word_tile", align_bytes=MX_ALIGN)
        w2_scale_tile = held.tile([P, H], U8, name="w2_scale_tile", align_bytes=MX_ALIGN)
        w1_mx = [operand("w1_%d" % a, KP) for a in range(2)]

        def deal_w2(dealt, loaded):
            nc.vector.tensor_copy(
                out=dealt.rearrange("p (a t m) -> p a t m", a=2, t=PACK),
                in_=loaded.rearrange("p (a m t) -> p a t m", a=2, t=PACK),
            )

        def pick_reports(half):
            cols = slice(half * BANK, (half + 1) * BANK)
            nc.vector.tensor_copy(v_scales[:, cols], table_scales[:].indirect(entries(list1, cols)))
            nc.vector.tensor_copy(v_words[:, cols], table_words[:].bitcast(U32).indirect(entries(list1, cols)))

        def dealt_w1(a):
            return w1_in[a][:].rearrange("p j (m t) -> p t m j", t=PACK)

        def quantise_w1_slice(t):
            woven = ring.tile([P, P, PACK], BF16, name="w1_woven", align_bytes=MX_ALIGN, bufs=PACK)
            nc.scalar.copy(out=woven[:], in_=dealt_w1(0)[:, t])
            cols = slice(t * P, (t + 1) * P)
            quantise((w1_mx[0][0][:, cols], w1_mx[0][1][:, cols]), woven[:].rearrange("p m j -> p (m j)"))

        deal_w2(w2_word_tile[:].bitcast(U16), w2_words_in[:].bitcast(U16))
        pick_reports(0)
        quantise_w1_slice(0)
        pick_reports(1)
        deal_w2(w2_scale_tile[:], w2_scales_in[:])

        w3_in = held.tile([P, 2, PACK, N], F32, name="w3_in", tag="table_words")
        for a in range(2):
            load_rows(w3_in[:, a], w3[a * KP : (a + 1) * KP, :])

        def products(s):
            a, t = divmod(s, PACK)
            cols_r = slice(t * P, (t + 1) * P)
            h1 = ring.tile([P, S], F32, name="h1")
            level = ring.tile([P, S], F32, name="level")
            for half in range(2):
                cols = slice(half * BANK, (half + 1) * BANK)
                acc = bank(half)
                nc.tensor.matmul_mx(
                    out=acc[:],
                    lhsT=w1_mx[a][0][:, cols_r].bitcast(FP8X4),
                    lhsT_scale=w1_mx[a][1][:, cols_r],
                    rhs=v_words[:, cols].bitcast(FP8X4),
                    rhs_scale=v_scales[:, cols],
                    start=True,
                    stop=True,
                )
                nc.scalar.copy(out=h1[:, cols], in_=acc[:])
            for half in range(2):
                cols = slice(half * BANK, (half + 1) * BANK)
                acc = bank(2 + half)
                nc.tensor.matmul_mx(
                    out=acc[:],
                    lhsT=w2_word_tile[:, 2 * P * s : 2 * P * (s + 1)].bitcast(FP4X4),
                    lhsT_scale=w2_scale_tile[:, P * s : P * (s + 1)],
                    rhs=v_words[:, cols].bitcast(FP8X4),
                    rhs_scale=v_scales[:, cols],
                    start=True,
                    stop=True,
                )
                nc.scalar.activation(out=level[:, cols], in_=acc[:], func=COPY, scale=gains[:, a, t : t + 1])
            return h1, level

        states = [held.tile([P, S], F32, name="state%d" % i, align_bytes=MX_ALIGN) for i in range(STATES)]

        def fetch_and_add(s, h1):
            pieces = 2 if s == 0 else 1
            for i in range(pieces):
                cols = slice(i * S // pieces, (i + 1) * S // pieces)
                nc.vector.tensor_tensor(
                    states[s % STATES][:, cols], pages[s][:].indirect(entries(list2, cols)), h1[:, cols], ADD
                )

        def keep_larger(s, level):
            state = states[s % STATES]
            nc.vector.tensor_tensor(state[:], state[:], level[:], MAX)

        def put_back(s):
            nc.vector.tensor_copy(pages[s][:].indirect(list2[:]), states[s % STATES][:])

        w5_mx = operand("w5", N)
        w3_mx = [operand("w3_%d" % a, N) for a in range(2)]
        staged = [
            (w1_mx[1], dealt_w1(1), "p (t m j) -> p t m j", {"t": PACK, "j": PACK}),
            (w5_mx, w5_in[:].rearrange("p j c -> p c j"), "p (c j) -> p c j", {"j": PACK}),
            (w3_mx[0], w3_in[:, 0].rearrange("p j c -> p c j"), "p (c j) -> p c j", {"j": PACK}),
            (w3_mx[1], w3_in[:, 1].rearrange("p j c -> p c j"), "p (c j) -> p c j", {"j": PACK}),
        ]

        def quantise_staged(s):
            (words, scales), source, view, sizes = staged[s]
            woven = states[s % STATES][:].bitcast(BF16)
            nc.scalar.copy(out=woven.rearrange(view, **sizes), in_=source)
            quantise((words[:], scales[:]), woven)

        x_mx = [
            [operand("x%d_%d" % (a, c), CHUNK, tag="x%d_%d" % (a, c)) for c in range(CHUNKS)] for a in range(2)
        ]
        planes_pass0 = held.tile([P, PACK, S], BF16, name="planes_pass0")

        def as_planes(tile):
            return tile[:].bitcast(BF16)[:, 0 : PACK * CHUNK].rearrange("p (t c) -> p t c", t=PACK)

        def fetch_planes(planes, c, which):
            cols = slice(c * CHUNK, (c + 1) * CHUNK)
            for t in which:
                nc.vector.tensor_copy(planes[:, t, :], pages[PACK + t][:].indirect(entries(list3, cols)))

        def quantise_x(a, c, planes, tile):
            woven = tile[:].bitcast(BF16)
            nc.scalar.copy(out=woven.rearrange("p (c t) -> p c t", t=PACK), in_=planes.rearrange("p t c -> p c t"))
            quantise((x_mx[a][c][0][:], x_mx[a][c][1][:]), woven)

        h1, level = products(0)
        for t in range(1, PACK):
            quantise_w1_slice(t)
        fetch_and_add(0, h1)
        keep_larger(0, level)
        planes = {}
        for s in range(SLICES):
            if s + 1 < SLICES:
                h1, level = products(s + 1)
                fetch_and_add(s + 1, h1)
            put_back(s)
            if s + 1 < SLICES:
                keep_larger(s + 1, level)
            if s < PACK:
                nc.vector.tensor_copy(planes_pass0[:, s, :], pages[s][:].indirect(list3[:]))
                quantise_staged(s)
            if s == PACK:
                for c in range(CHUNKS):
                    tile = ring.tile([P, 2 * CHUNK], U32, name="x0_woven", align_bytes=MX_ALIGN, bufs=CHUNKS)
                    quantise_x(0, c, planes_pass0[:, :, c * CHUNK : (c + 1) * CHUNK], tile)
            if s == SLICES - 2:
                planes[0] = as_planes(states[s % STATES])
                fetch_planes(planes[0], 0, range(PACK - 1))

        def mx_pass(acc, i, lhs_words, lhs_scales, rhs_words, rhs_scales, start, stop):
            nc.tensor.matmul_mx(
                out=acc[:, i * CHUNK : (i + 1) * CHUNK],
                lhsT=lhs_words,
                lhsT_scale=lhs_scales,
                rhs=rhs_words.bitcast(FP8X4),
                rhs_scale=rhs_scales,
                start=start,
                stop=stop,
            )

        def w5_pass(acc, i, c, pair, start, stop):
            n = slice((2 * pair + i) * P, (2 * pair + i + 1) * P)
            cols = slice(c * CHUNK, (c + 1) * CHUNK)
            mx_pass(acc, i, w5_mx[0][:, n].bitcast(FP8X4), w5_mx[1][:, n], v_words[:, cols], v_scales[:, cols], start, stop)

        def w3_pass(acc, i, c, pair, a, start, stop):
            n = slice((2 * pair + i) * P, (2 * pair + i + 1) * P)
            words, scales = x_mx[a][c]
            mx_pass(acc, i, w3_mx[a][0][:, n].bitcast(FP8X4), w3_mx[a][1][:, n], words[:], scales[:], start, stop)

        def w4_pass(acc, i, c, pair, a, start, stop):
            n = slice((2 * pair + i) * P, (2 * pair + i + 1) * P)
            words, scales = x_mx[a][c]
            lhs = w4_word_tile[:, a, 2 * n.start : 2 * n.stop].bitcast(FP4X4)
            mx_pass(acc, i, lhs, w4_scale_tile[:, a, n], words[:], scales[:], start, stop)

        acc = bank(4)
        for i in range(2):
            w5_pass(acc, i, *ADDED_AFTER, True, True)
        skip = held.tile([P, BANK], F32, name="skip")
        nc.scalar.copy(out=skip[:], in_=acc[:])

        def open_chunk(c):
            first = 4 * ((c + 1) % 2)
            accs = []
            for pair in range(2):
                acc_a, acc_b = bank(first + 2 * pair), bank(first + 2 * pair + 1)
                inside = (c, pair) != ADDED_AFTER
                for acc, product in ((acc_b, w4_pass), (acc_a, w3_pass)):
                    for i in range(2):
                        if inside:
                            w5_pass(acc, i, c, pair, i == 0, False)
                        product(acc, i, c, pair, 0, i == 0 and not inside, False)
                accs.append((acc_a, acc_b))
            return accs

        def close_chunk(c, accs):
            sums = []
            for pair in range(2):
                acc_a, acc_b = accs[pair]
                for acc, product in ((acc_b, w4_pass), (acc_a, w3_pass)):
                    for i in range(2):
                        product(acc, i, c, pair, 1, False, i == 1)
                y_b = ring.tile([P, BANK], F32, name="y_b", bufs=4)
                nc.scalar.copy(out=y_b[:], in_=acc_b[:])
                y_a = acc_a
                if c < 2:
                    y_a = ring.tile([P, BANK], F32, name="y_a", bufs=4)
                    nc.scalar.copy(out=y_a[:], in_=acc_a[:])
                sums.append((y_a, y_b))
            return sums

        def finish_chunk(c, sums):
            for pair in range(2):
                y_a, y_b = sums[pair]
                if (c, pair) == (0, 0):
                    result = held.tile([P, BANK], F32, name="result", tag="x1_0", align_bytes=MX_ALIGN)
                else:
                    result = ring.tile([P, BANK], F32, name="result", bufs=4)
                nc.vector.tensor_tensor(result[:], y_a[:], y_b[:], MAX)
                if (c, pair) == ADDED_AFTER:
                    nc.vector.tensor_tensor(result[:], result[:], skip[:], ADD)
                rows = out[2 * pair * P : 2 * (pair + 1) * P, c * CHUNK : (c + 1) * CHUNK]
                nc.sync.dma_start(
                    out=rows.rearrange("(i p) c -> p i c", i=2), in_=result[:].rearrange("p (i c) -> p i c", i=2)
                )

        woven_x1 = [held.tile([P, 2 * CHUNK], U32, name="x1_woven%d" % c, align_bytes=MX_ALIGN) for c in range(2)]
        accs = {0: open_chunk(0), 1: open_chunk(1)}
        fetch_planes(planes[0], 0, [PACK - 1])
        planes[1] = as_planes(states[(SLICES - 1) % STATES])
        fetch_planes(planes[1], 1, range(PACK))
        sums = {}

        def quantise_late(c):
            tile = held.tile([P, 2 * CHUNK], U32, name="x1_woven", tag="x1_%d" % (c - 2), align_bytes=MX_ALIGN)
            quantise_x(1, c, planes[c], tile)

        for c in range(2):
            quantise_x(1, c, planes[c], woven_x1[c])
            planes[c + 2] = as_planes(woven_x1[c])
            fetch_planes(planes[c + 2], c + 2, range(PACK))
            if c == 1:
                quantise_late(2)
            sums[c] = close_chunk(c, accs[c])
            accs[c + 2] = open_chunk(c + 2)
        quantise_late(3)
        for c in range(CHUNKS):
            if c >= 2:
                sums[c] = close_chunk(c, accs[c])
            finish_chunk(c, sums[c])
